import numpy as np
import ml_dtypes


def mxq(x, axis, fmt="e4m3"):
    dtype, down = {"e4m3": (ml_dtypes.float8_e4m3fn, 7), "e5m2": (ml_dtypes.float8_e5m2, 14)}[fmt]
    v = np.moveaxis(np.asarray(x, np.float32).astype(ml_dtypes.bfloat16).astype(np.float64), axis, -1)
    blocks = v.reshape(v.shape[:-1] + (-1, 32))
    amax = np.abs(blocks).max(-1, keepdims=True)
    byte = np.maximum(np.where(amax > 0, np.frexp(amax)[1] - 1 + 127, 0) - down, 1)
    scale = np.exp2(byte - 127.0)
    codes = (blocks / scale).astype(np.float32).astype(dtype).astype(np.float64)
    return np.moveaxis((codes * scale).reshape(v.shape), -1, axis)


WIDE = False


def mx_kscale(k):
    if not WIDE:
        return np.ones(k)
    levels = np.array([10, -10, 5, -5, 0])
    if k % 512:
        return np.exp2(np.random.permutation(np.resize(levels, k // 32))).repeat(32)
    a = np.empty((k // 512, 16))
    for p in range(k // 512):
        a[p, :8] = np.random.permutation(np.resize(levels, 8))
        for g in range(8):
            far = levels[np.abs(levels - a[p, g]) >= 10]
            a[p, g + 8] = far[np.random.randint(len(far))]
    return np.exp2(a.ravel()).repeat(32)


BF16 = ml_dtypes.bfloat16


def bf(x):
    return np.asarray(x, np.float32).astype(BF16)


def f64(x):
    return np.asarray(x).astype(np.float64)


E2M1 = np.array([0.0, 0.5, 1.0, 1.5, 2.0, 3.0, 4.0, 6.0, -0.0, -0.5, -1.0, -1.5, -2.0, -3.0, -4.0, -6.0])


def pack_weight(w, fmt):
    k, n = w.shape
    w = f64(bf(w)).reshape(k // 32, 32, n)
    amax = np.abs(w).max(1)
    if fmt == "e4m3":
        byte = np.frexp(amax)[1] - 1 + 127 - 7
    else:
        mant, ex = np.frexp(amax / 6.0)
        byte = np.where(mant > 0.5, ex, ex - 1) + 127
    byte = np.clip(np.where(amax > 0, byte, 1), 1, 254)
    scaled = (w * np.exp2(127.0 - byte)[:, None, :]).reshape(k, n).astype(np.float32)
    by_word = np.ascontiguousarray(scaled.reshape(k // 512, 128, 4, n).transpose(0, 1, 3, 2))
    if fmt == "e4m3":
        words = by_word.astype(ml_dtypes.float8_e4m3fn).view(np.uint8)
    else:
        c = by_word.astype(ml_dtypes.float4_e2m1fn).view(np.uint8) & 0xF
        words = c[..., 0::2] | (c[..., 1::2] << 4)
    return np.ascontiguousarray(words), np.ascontiguousarray(byte.astype(np.uint8).reshape(k // 512, 16, n))


def unpack_weight(words, scales, fmt):
    g, p, n, _ = words.shape
    if fmt == "e4m3":
        vals = np.ascontiguousarray(words).view(ml_dtypes.float8_e4m3fn).astype(np.float64)
    else:
        nib = np.empty((g, p, n, 4), np.uint8)
        nib[..., 0::2] = words & 0xF
        nib[..., 1::2] = words >> 4
        vals = E2M1[nib]
    vals = vals * np.repeat(np.exp2(scales.astype(np.float64) - 127.0), 8, axis=1)[..., None]
    return vals.transpose(0, 1, 3, 2).reshape(g * 512, n)


N, D = 2048, 1024


def draw0():
    s, t = mx_kscale(D), mx_kscale(N)
    x = np.random.standard_normal((N, D)) * s
    w = np.random.standard_normal((D, D)) / np.sqrt(D) / s[None, :]
    k = np.random.uniform(-1.0, 1.0, D)
    g = (1.0 + 0.1 * np.random.standard_normal(N)) * t
    h = (1.0 + 0.1 * np.random.standard_normal(N)) / t
    words, scales = pack_weight(w.T, "e4m3")
    return {"x": bf(x), "w_words": words, "w_scales": scales, "k": bf(k), "g": bf(g), "h": bf(h)}


def core(x, w_words, w_scales, k, g, h):
    n = x.shape[0]
    root_n = np.sqrt(n)
    y = mxq(f64(x), 1, "e4m3") @ unpack_weight(w_words, w_scales, "e4m3")
    p = f64(g)[:, None] * (f64(k)[None, :] * np.tanh(y) + y)
    z = f64(h)[:, None] * y
    c = (mxq(p, 0, "e4m3").T @ mxq(z, 0, "e4m3")) / root_n
    return root_n * np.eye(w_words.shape[2]) - c


def e4m3fn_bytes(y):
    return np.clip(np.asarray(y, np.float64), -448.0, 448.0).astype(np.float32).astype(ml_dtypes.float8_e4m3fn).view(np.uint8)


def e4m3fn_values(b):
    return np.asarray(b, np.uint8).view(ml_dtypes.float8_e4m3fn).astype(np.float64)


def setup_inputs():
    d = draw0()
    x0 = np.asarray(d['x']).astype(np.float64)
    s = (np.max(np.abs(x0), axis=(0,), keepdims=True) / 448.0).astype(np.float32)
    out = {}
    for k, v in d.items():
        if k == 'x':
            out['x_bytes'] = e4m3fn_bytes(x0 / s.astype(np.float64))
            out['x_scale'] = s
        else:
            out[k] = v
    return out


def reference(x_bytes, x_scale, w_words, w_scales, k, g, h):
    return core(e4m3fn_values(x_bytes) * x_scale.astype(np.float64), w_words, w_scales, k, g, h)

@@ -1,0 +1,357 @@
+import math
+from contextlib import ExitStack
+
+import concourse.mybir as mybir
+from concourse.masks import make_identity
+
+N, D = 2048, 1024
+P = 128
+PACK = 4
+GROUP = P * PACK
+NG = N // GROUP
+KG = D // GROUP
+BANK = 512
+ROOT = math.sqrt(N)
+
+FLOPS = 4 * N * D * D
+
+F32 = mybir.dt.float32
+BF16 = mybir.dt.bfloat16
+U32 = mybir.dt.uint32
+I32 = mybir.dt.int32
+U8 = mybir.dt.uint8
+FP8 = mybir.dt.float8_e4m3fn
+X4 = mybir.dt.float8_e4m3fn_x4
+ALU = mybir.AluOpType
+ACT = mybir.ActivationFunctionType
+
+BLOCKS = [(0, 512), (512, 256), (768, 256)]
+SHARE = 4
+
+
+def tile_extendedinfomaxnaturalgradient_w8_kernel(tc, x_bytes, x_scale, w_words, w_scales, k, g, h, out):
+    nc = tc.nc
+    with ExitStack() as ctx:
+        keep = ctx.enter_context(tc.tile_pool(name="keep", bufs=1))
+        work = ctx.enter_context(tc.tile_pool(name="work", bufs=2))
+        psum = ctx.enter_context(tc.psum_pool(name="psum", bufs=4))
+        ctx.enter_context(tc.manual_schedule())
+
+        warm = keep.tile([P, 1], F32, name="warm")
+        nc.vector.memset(warm[:], 0.0)
+        warm_out = keep.tile([P, 1], F32, name="warm_out")
+        nc.scalar.activation(warm_out[:], warm[:], ACT.Tanh)
+
+        w_sc = keep.tile([P, KG, D], U8, name="w_sc", align_bytes=64)
+        nc.vector.memset(w_sc[:].rearrange("p g n -> p (g n)").bitcast(I32), 0)
+
+        ident = keep.tile([P, P], F32, name="ident")
+        make_identity(nc, ident[:])
+
+        gh_bf = keep.tile([P, 2, NG, PACK], BF16, name="gh_bf")
+        with nc.allow_non_contiguous_dma(reason="gains: four neighbouring samples a piece"):
+            nc.gpsimd.dma_start(out=gh_bf[:, 0], in_=g.rearrange("(q m t) -> m q t", m=P, t=PACK))
+            nc.gpsimd.dma_start(out=gh_bf[:, 1], in_=h.rearrange("(q m t) -> m q t", m=P, t=PACK))
+        k_bc = keep.tile([P, D], BF16, name="k_bc")
+        nc.gpsimd.dma_start(out=k_bc[:], in_=k.partition_broadcast(P))
+
+        x_view = x_bytes.rearrange("(q m t) k -> q m (t k)", m=P, t=PACK)
+        xb = [keep.tile([P, PACK * D], U8, name=f"xb{q}") for q in range(NG)]
+        half = PACK * D // 2
+        xs = keep.tile([P, D], F32, name="xs")
+        w_codes = keep.tile([P, KG, D], U32, name="w_codes", align_bytes=64)
+        w_view = [w_words[c].rearrange("p n t -> p (n t)").bitcast(I32) for c in range(KG)]
+        xs_row = x_scale.rearrange("o k -> (o k)")
+        nc.sync.dma_start(out=xs[:, :BANK], in_=xs_row[:BANK].partition_broadcast(P))
+        nc.sync.dma_start(out=xb[0][:, :half], in_=x_view[0][:, :half])
+        nc.sync.dma_start(out=xs[:, BANK:], in_=xs_row[BANK:].partition_broadcast(P))
+        nc.sync.dma_start(out=xb[0][:, half:], in_=x_view[0][:, half:])
+        nc.sync.dma_start(out=xb[1][:], in_=x_view[1])
+        for c in range(KG):
+            for j in range(PACK):
+                nc.sync.dma_start(out=w_sc[j:P:32, c, :].bitcast(I32), in_=w_scales[c, j:16:4, :].bitcast(I32))
+        for c in range(KG):
+            nc.sync.dma_start(out=w_codes[:, c, :BANK].bitcast(I32), in_=w_view[c][:, :BANK])
+        for c in range(KG):
+            nc.sync.dma_start(out=w_codes[:, c, BANK:].bitcast(I32), in_=w_view[c][:, BANK:])
+        for q in range(2, NG):
+            nc.sync.dma_start(out=xb[q][:], in_=x_view[q])
+
+        gh = keep.tile([P, 2, NG, PACK], F32, name="gh")
+        root_i = keep.tile([P, P], F32, name="root_i")
+
+        x_codes = [keep.tile([P, KG, GROUP], U32, name=f"x_codes{q}", align_bytes=64) for q in range(NG)]
+        x_sc = [keep.tile([P, KG, GROUP], U8, name=f"x_sc{q}", align_bytes=64) for q in range(NG)]
+        p_codes = keep.tile([P, NG, D], U32, name="p_codes", align_bytes=64)
+        p_sc = keep.tile([P, NG, D], U8, name="p_sc", align_bytes=64)
+        z_codes = keep.tile([P, NG, D], U32, name="z_codes", align_bytes=64)
+        z_sc = keep.tile([P, NG, D], U8, name="z_sc", align_bytes=64)
+
+        xv = {}
+        xg = {}
+
+        def widen(q, t, lo=0, hi=D):
+            if lo == 0:
+                xv[q, t] = work.tile([P, D], BF16, name="xv", bufs=6)
+            nc.vector.tensor_tensor(xv[q, t][:, lo:hi], xb[q][:, t * D + lo:t * D + hi].bitcast(FP8), xs[:, lo:hi], ALU.mult)
+
+        xt = {}
+
+        def turn(q, c, pair):
+            b = psum.tile([P, 2, 2, P], F32, name="wk")
+            for a in range(2):
+                words = xv[q, 2 * pair + a][:].bitcast(F32)
+                for u in range(2):
+                    nc.tensor.transpose(b[:, a, u, :], words[:, 256 * c + u:256 * (c + 1):2], ident[:])
+            xt[q, c, pair] = b
+
+        def untank(q, c, pair):
+            if pair == 0:
+                xg[q, c] = work.tile([P, GROUP * PACK], BF16, name=f"xg{c}", align_bytes=64)
+            dst = xg[q, c][:].bitcast(F32)[:, pair * BANK:(pair + 1) * BANK]
+            nc.scalar.copy(dst.rearrange("p (a r u) -> p a r u", a=2, u=2), xt[q, c, pair][:].rearrange("p a u r -> p a r u"))
+
+        def quant_x(q, c):
+            nc.vector.quantize_mx(out=x_codes[q][:, c, :].bitcast(X4), scales=x_sc[q][:, c, :], in_=xg[q, c][:])
+
+        y = {}
+        th = {}
+        aa = {}
+        pp = {}
+        zp = {}
+        pi = {}
+        zi = {}
+
+        def project(b, q, j):
+            c0, cw = BLOCKS[b]
+            nt = BANK // cw
+            bank = psum.tile([P, nt, cw], F32, name="y", bufs=4)
+            for a in range(nt):
+                t = j * nt + a
+                for c in range(KG):
+                    nc.tensor.matmul_mx(
+                        out=bank[:, a, :],
+                        lhsT=x_codes[q][:, c, t * P:(t + 1) * P].bitcast(X4),
+                        lhsT_scale=x_sc[q][:, c, t * P:(t + 1) * P],
+                        rhs=w_codes[:, c, c0:c0 + cw].bitcast(X4),
+                        rhs_scale=w_sc[:, c, c0:c0 + cw],
+                        start=(c == 0), stop=(c == KG - 1))
+                y[b, q, t] = bank[:, a, :]
+            y[b, q, "bank", j] = bank
+
+        def start_e(b, q):
+            cw = BLOCKS[b][1]
+            pp[b, q] = work.tile([P, PACK, cw], BF16, name="pp", bufs=3, align_bytes=64)
+            zp[b, q] = work.tile([P, PACK, cw], BF16, name="zp", bufs=3, align_bytes=64)
+
+        def scalar_e(b, q, j):
+            cw = BLOCKS[b][1]
+            nt = BANK // cw
+            tt = work.tile([P, nt, cw], F32, name="th", bufs=4)
+            nc.scalar.activation(tt[:], y[b, q, "bank", j][:], ACT.Tanh)
+            for a in range(nt):
+                t = j * nt + a
+                th[b, q, t] = tt[:, a, :]
+                nc.scalar.activation(zp[b, q][:, t, :], y[b, q, t], ACT.Copy, scale=gh[:, 1, q, t:t + 1])
+
+        def vec_a(b, q, t):
+            c0, cw = BLOCKS[b][0], BLOCKS[b][1]
+            a = work.tile([P, cw], F32, name="aa", bufs=4)
+            nc.vector.scalar_tensor_tensor(a[:], th[b, q, t], gh[:, 0, q, t:t + 1], k_bc[:, c0:c0 + cw], ALU.mult, ALU.mult)
+            aa[b, q, t] = a
+
+        def vec_p(b, q, t):
+            nc.vector.scalar_tensor_tensor(pp[b, q][:, t, :], y[b, q, t], gh[:, 0, q, t:t + 1], aa[b, q, t][:], ALU.mult, ALU.add)
+
+        def inter(kind, b, q, eng, lo, hi):
+            src = (zp if kind == "z" else pp)[b, q]
+            dst = zi if kind == "z" else pi
+            if (b, q) not in dst:
+                dst[b, q] = work.tile([P, BLOCKS[b][1] * PACK], BF16, name=kind + "i", bufs=3, align_bytes=64)
+            o = dst[b, q][:, lo * PACK:hi * PACK].rearrange("p (c i t) -> p c t i", i=4, t=PACK)
+            s = src[:, :, lo:hi].rearrange("p t (c i) -> p c t i", i=4)
+            if eng == "s":
+                nc.scalar.copy(o, s)
+            else:
+                nc.vector.tensor_copy(out=o, in_=s)
+
+        def quant(kind, b, q):
+            c0, cw = BLOCKS[b][0], BLOCKS[b][1]
+            codes, sc, src = (z_codes, z_sc, zi) if kind == "z" else (p_codes, p_sc, pi)
+            nc.vector.quantize_mx(out=codes[:, q, c0:c0 + cw].bitcast(X4), scales=sc[:, q, c0:c0 + cw], in_=src[b, q][:])
+
+        def cross_pass(dst, mi, n0, nw, q):
+            nc.tensor.matmul_mx(
+                out=dst,
+                lhsT=p_codes[:, q, mi * P:(mi + 1) * P].bitcast(X4), lhsT_scale=p_sc[:, q, mi * P:(mi + 1) * P],
+                rhs=z_codes[:, q, n0:n0 + nw].bitcast(X4), rhs_scale=z_sc[:, q, n0:n0 + nw],
+                start=(q == 0), stop=(q == NG - 1))
+
+        def cross(mi, n0, nw, tag="wk"):
+            nm = BANK // nw
+            bank = psum.tile([P, nm, nw], F32, name=tag)
+            for a in range(nm):
+                for q in range(NG):
+                    cross_pass(bank[:, a, :], mi + a, n0, nw, q)
+            return bank
+
+        def leave(bank, mi, n0, nw, eng):
+            nm = BANK // nw
+            o = work.tile([P, nm, nw], F32, name="o", bufs=8)
+            if eng == "s":
+                nc.scalar.activation(o[:], bank[:], ACT.Copy, scale=-1.0 / ROOT)
+            else:
+                nc.vector.tensor_scalar(o[:], bank[:], -1.0 / ROOT, None, ALU.mult)
+            return o, mi, n0, nw
+
+        def store(o, mi, n0, nw):
+            nm = BANK // nw
+            for a in range(nm):
+                d = (mi + a) * P - n0
+                if 0 <= d < nw:
+                    nc.vector.tensor_tensor(o[:, a, d:d + P], o[:, a, d:d + P], root_i[:], ALU.add)
+            nc.sync.dma_start(
+                out=out[mi * P:(mi + nm) * P, n0:n0 + nw].rearrange("(a m) n -> m a n", m=P), in_=o[:])
+
+        steps = [(b, q) for b in range(len(BLOCKS)) for q in range(NG)]
+        jobs = {
+            5: [(0, 0, 512, "s")], 6: [(1, 0, 512, "s"), (2, 0, 512, "s")], 7: [(3, 0, 512, "s")],
+            9: [(0, 512, 256, "s"), (2, 512, 256, "s"), (4, 512, 256, "s")], 10: [(4, 0, 512, "s"), (5, 0, 512, "s")],
+        }
+
+        def turn_pair(q, pair):
+            for c in range(KG):
+                turn(q, c, pair)
+
+        def untank_pair(q, pair):
+            for c in range(KG):
+                untank(q, c, pair)
+
+        for pair in range(2):
+            for c in range(KG):
+                widen(0, 2 * pair, c * BANK, (c + 1) * BANK)
+                widen(0, 2 * pair + 1, c * BANK, (c + 1) * BANK)
+                turn(0, c, pair)
+                untank(0, c, pair)
+        nc.vector.tensor_copy(out=gh[:], in_=gh_bf[:])
+        nc.vector.tensor_scalar(root_i[:], ident[:], ROOT, None, ALU.mult)
+        widen(1, 0)
+        quant_x(0, 0)
+        quant_x(0, 1)
+        for j in range(PACK):
+            project(0, 0, j)
+
+        open_banks = {}
+
+        def open_all(qq):
+            for mi in (6, 7):
+                for n0 in (0, 512):
+                    if qq == 0:
+                        open_banks[mi, n0] = psum.tile([P, 1, BANK], F32, name="wk")
+                    cross_pass(open_banks[mi, n0][:, 0, :], mi, n0, BANK, qq)
+
+        late = None
+        done = []
+        for s, (b, q) in enumerate(steps):
+            prev = steps[s - 1] if s else None
+            follow = steps[s + 1] if s + 1 < len(steps) else None
+            start_e(b, q)
+            if b == 0:
+                more = q + 1 < NG
+                scalar_e(b, q, 0)
+                if more:
+                    widen(q + 1, 1)
+                    turn_pair(q + 1, 0)
+                if late:
+                    quant("p", *late)
+                vec_a(b, q, 0)
+                scalar_e(b, q, 1)
+                if prev:
+                    inter("z", *prev, "s", 0, 256)
+                if more:
+                    untank_pair(q + 1, 0)
+                    widen(q + 1, 2)
+                vec_p(b, q, 0)
+                vec_a(b, q, 1)
+                scalar_e(b, q, 2)
+                if prev:
+                    inter("z", *prev, "s", 256, 512)
+                if more:
+                    widen(q + 1, 3)
+                    turn_pair(q + 1, 1)
+                    untank_pair(q + 1, 1)
+                vec_p(b, q, 1)
+                vec_a(b, q, 2)
+                if more:
+                    quant_x(q + 1, 0)
+                scalar_e(b, q, 3)
+                vec_p(b, q, 2)
+                if more:
+                    quant_x(q + 1, 1)
+                    project(*follow, 0)
+                    project(*follow, 1)
+                    project(*follow, 2)
+                if prev:
+                    inter("p", *prev, "s", 0, 256)
+                    inter("p", *prev, "s", 256, 512)
+                vec_a(b, q, 3)
+                if q + 2 < NG:
+                    widen(q + 2, 0)
+                if prev:
+                    quant("z", *prev)
+                vec_p(b, q, 3)
+                if more:
+                    project(*follow, 3)
+                else:
+                    project(*follow, 0)
+                    project(*follow, 1)
+            else:
+                for item in done:
+                    store(*item)
+                done = []
+                w = BLOCKS[prev[0]][1]
+                cut = w * SHARE // 16 if follow else w
+                scalar_e(b, q, 0)
+                if not follow:
+                    inter("p", *prev, "v", 0, w)
+                inter("z", *prev, "v", 0, w)
+                if late:
+                    quant("p", *late)
+                scalar_e(b, q, 1)
+                if not follow:
+                    open_all(0)
+                    open_all(1)
+                    inter("z", *steps[s], "s", 0, BLOCKS[b][1])
+                vec_a(b, q, 0)
+                vec_a(b, q, 1)
+                vec_p(b, q, 0)
+                vec_a(b, q, 2)
+                vec_p(b, q, 1)
+                quant("z", *prev)
+                if not follow:
+                    quant("p", *prev)
+                vec_a(b, q, 3)
+                vec_p(b, q, 2)
+                if follow:
+                    if cut:
+                        inter("p", *prev, "v", 0, cut)
+                    inter("p", *prev, "s", cut, w)
+                else:
+                    quant("z", *steps[s])
+                vec_p(b, q, 3)
+                if follow:
+                    project(*follow, 0)
+                    project(*follow, 1)
+                for mi, n0, nw, eng in jobs.get(s, []):
+                    done.append(leave(cross(mi, n0, nw), mi, n0, nw, eng))
+            late = prev
+        last = steps[-1]
+        w = BLOCKS[-1][1]
+        open_all(2)
+        inter("p", *last, "v", 0, w)
+        quant("p", *last)
+        for i, mi in enumerate((0, 2, 4)):
+            store(*leave(cross(mi, 768, 256, "y"), mi, 768, 256, "sv"[i % 2]))
+        for i, (mi, n0) in enumerate(open_banks):
+            cross_pass(open_banks[mi, n0][:, 0, :], mi, n0, BANK, NG - 1)
+            store(*leave(open_banks[mi, n0], mi, n0, BANK, "vs"[i % 2]))

@@ -26,6 +26,8 @@ ALU = mybir.AluOpType
 ACT = mybir.ActivationFunctionType
 
 BLOCKS = [(0, 512), (512, 256), (768, 256)]
+ZSHARE = 16
+CUT3 = 512
 SHARE = 4
 
 
@@ -48,12 +50,16 @@ def tile_extendedinfomaxnaturalgradient_w8_kernel(tc, x_bytes, x_scale, w_words,
         ident = keep.tile([P, P], F32, name="ident")
         make_identity(nc, ident[:])
 
+        k_row = keep.tile([P, D], BF16, name="k_row")
+        nc.vector.memset(k_row[:].bitcast(I32), 0)
+        nc.scalar.dma_start(out=k_row[0:1, :], in_=k.rearrange("(o n) -> o n", o=1))
         gh_bf = keep.tile([P, 2, NG, PACK], BF16, name="gh_bf")
         with nc.allow_non_contiguous_dma(reason="gains: four neighbouring samples a piece"):
-            nc.gpsimd.dma_start(out=gh_bf[:, 0], in_=g.rearrange("(q m t) -> m q t", m=P, t=PACK))
-            nc.gpsimd.dma_start(out=gh_bf[:, 1], in_=h.rearrange("(q m t) -> m q t", m=P, t=PACK))
+            nc.scalar.dma_start(out=gh_bf[:, 0], in_=g.rearrange("(q m t) -> m q t", m=P, t=PACK))
+            nc.scalar.dma_start(out=gh_bf[:, 1], in_=h.rearrange("(q m t) -> m q t", m=P, t=PACK))
+        ones = keep.tile([P, P], BF16, name="ones")
+        nc.vector.memset(ones[:], 1.0)
         k_bc = keep.tile([P, D], BF16, name="k_bc")
-        nc.gpsimd.dma_start(out=k_bc[:], in_=k.partition_broadcast(P))
 
         x_view = x_bytes.rearrange("(q m t) k -> q m (t k)", m=P, t=PACK)
         xb = [keep.tile([P, PACK * D], U8, name=f"xb{q}") for q in range(NG)]
@@ -61,17 +67,18 @@ def tile_extendedinfomaxnaturalgradient_w8_kernel(tc, x_bytes, x_scale, w_words,
         xs = keep.tile([P, D], F32, name="xs")
         w_codes = keep.tile([P, KG, D], U32, name="w_codes", align_bytes=64)
         w_view = [w_words[c].rearrange("p n t -> p (n t)").bitcast(I32) for c in range(KG)]
-        xs_row = x_scale.rearrange("o k -> (o k)")
-        nc.sync.dma_start(out=xs[:, :BANK], in_=xs_row[:BANK].partition_broadcast(P))
-        nc.sync.dma_start(out=xb[0][:, :half], in_=x_view[0][:, :half])
-        nc.sync.dma_start(out=xs[:, BANK:], in_=xs_row[BANK:].partition_broadcast(P))
+        xs_col = keep.tile([P, KG, PACK], F32, name="xs_col")
+        for t in range(PACK // 2):
+            nc.sync.dma_start(out=xb[0][:, t * D:(t + 1) * D], in_=x_view[0][:, t * D:(t + 1) * D])
+        nc.sync.dma_start(out=xs_col[:], in_=x_scale.rearrange("o (c p t) -> p (o c) t", p=P, t=PACK))
         nc.sync.dma_start(out=xb[0][:, half:], in_=x_view[0][:, half:])
-        nc.sync.dma_start(out=xb[1][:], in_=x_view[1])
-        for c in range(KG):
-            for j in range(PACK):
-                nc.sync.dma_start(out=w_sc[j:P:32, c, :].bitcast(I32), in_=w_scales[c, j:16:4, :].bitcast(I32))
+        for j in range(PACK):
+            nc.sync.dma_start(
+                out=w_sc[j:P:32, :, :].bitcast(I32),
+                in_=w_scales[:, j:16:4, :].rearrange("c q n -> q c n").bitcast(I32))
         for c in range(KG):
             nc.sync.dma_start(out=w_codes[:, c, :BANK].bitcast(I32), in_=w_view[c][:, :BANK])
+        nc.sync.dma_start(out=xb[1][:], in_=x_view[1])
         for c in range(KG):
             nc.sync.dma_start(out=w_codes[:, c, BANK:].bitcast(I32), in_=w_view[c][:, BANK:])
         for q in range(2, NG):
@@ -90,29 +97,59 @@ def tile_extendedinfomaxnaturalgradient_w8_kernel(tc, x_bytes, x_scale, w_words,
         xv = {}
         xg = {}
 
-        def widen(q, t, lo=0, hi=D):
-            if lo == 0:
-                xv[q, t] = work.tile([P, D], BF16, name="xv", bufs=6)
-            nc.vector.tensor_tensor(xv[q, t][:, lo:hi], xb[q][:, t * D + lo:t * D + hi].bitcast(FP8), xs[:, lo:hi], ALU.mult)
+        def widen(q, t):
+            xv[q, t] = work.tile([P, D], BF16, name="xv", bufs=6)
+            nc.vector.tensor_tensor(xv[q, t][:], xb[q][:, t * D:(t + 1) * D].bitcast(FP8), xs[:], ALU.mult)
 
         xt = {}
 
         def turn(q, c, pair):
-            b = psum.tile([P, 2, 2, P], F32, name="wk")
+            b = psum.tile([P, 2, 2 * P], F32, name="wk")
             for a in range(2):
                 words = xv[q, 2 * pair + a][:].bitcast(F32)
                 for u in range(2):
-                    nc.tensor.transpose(b[:, a, u, :], words[:, 256 * c + u:256 * (c + 1):2], ident[:])
+                    nc.tensor.transpose(b[:, u, a * P:(a + 1) * P], words[:, 256 * c + u:256 * (c + 1):2], ident[:])
             xt[q, c, pair] = b
 
-        def untank(q, c, pair):
+        def grouped(q, c, pair):
             if pair == 0:
                 xg[q, c] = work.tile([P, GROUP * PACK], BF16, name=f"xg{c}", align_bytes=64)
-            dst = xg[q, c][:].bitcast(F32)[:, pair * BANK:(pair + 1) * BANK]
-            nc.scalar.copy(dst.rearrange("p (a r u) -> p a r u", a=2, u=2), xt[q, c, pair][:].rearrange("p a u r -> p a r u"))
+            return xg[q, c][:, pair * 1024:(pair + 1) * 1024]
 
-        def quant_x(q, c):
-            nc.vector.quantize_mx(out=x_codes[q][:, c, :].bitcast(X4), scales=x_sc[q][:, c, :], in_=xg[q, c][:])
+        def untank(q, c, pair):
+            dst = grouped(q, c, pair).bitcast(F32)
+            nc.scalar.copy(dst.rearrange("p (r u) -> p r u", u=2), xt[q, c, pair][:].rearrange("p u r -> p r u"))
+
+        def widen_first(t, eng):
+            xv[0, t] = work.tile([P, D], BF16, name="xv", bufs=6)
+            byte = xb[0][:, t * D:(t + 1) * D].bitcast(FP8)
+            if eng == "s":
+                nc.scalar.copy(xv[0, t][:], byte)
+            else:
+                nc.vector.tensor_copy(out=xv[0, t][:], in_=byte)
+
+        def scale_first(c, pair):
+            nc.vector.tensor_tensor(
+                grouped(0, c, pair).rearrange("p (r u e) -> p r u e", u=2, e=2),
+                xt[0, c, pair][:].bitcast(BF16).rearrange("p u (r e) -> p r u e", e=2),
+                xs_col[:, c, :].rearrange("p (o u e) -> p o u e", o=1, u=2).broadcast_to([P, 2 * P, 2, 2]),
+                ALU.mult)
+
+        def spread_scale(c):
+            bank = psum.tile([P, PACK, P], F32, name="y")
+            for t in range(PACK):
+                nc.tensor.matmul(bank[:, t, :], lhsT=xs_col[:, c, t:t + 1].to_broadcast([P, P]), rhs=ident[:], start=True, stop=True)
+            nc.scalar.copy(
+                xs[:, c * GROUP:(c + 1) * GROUP].rearrange("p (n t) -> p n t", t=PACK), bank[:].rearrange("p t n -> p n t"))
+
+        def spread_k(c):
+            bank = psum.tile([P, BANK], F32, name="y")
+            nc.tensor.matmul(bank[:], lhsT=ones[:], rhs=k_row[:, c * BANK:(c + 1) * BANK], start=True, stop=True)
+            nc.scalar.copy(k_bc[:, c * BANK:(c + 1) * BANK], bank[:])
+
+        def quant_x(q, c, lo=0, hi=GROUP):
+            nc.vector.quantize_mx(
+                out=x_codes[q][:, c, lo:hi].bitcast(X4), scales=x_sc[q][:, c, lo:hi], in_=xg[q, c][:, lo * PACK:hi * PACK])
 
         y = {}
         th = {}
@@ -227,19 +264,28 @@ def tile_extendedinfomaxnaturalgradient_w8_kernel(tc, x_bytes, x_scale, w_words,
             for c in range(KG):
                 untank(q, c, pair)
 
-        for pair in range(2):
-            for c in range(KG):
-                widen(0, 2 * pair, c * BANK, (c + 1) * BANK)
-                widen(0, 2 * pair + 1, c * BANK, (c + 1) * BANK)
-                turn(0, c, pair)
-                untank(0, c, pair)
+        widen_first(0, "s")
+        widen_first(1, "v")
+        turn_pair(0, 0)
+        widen_first(2, "s")
+        widen_first(3, "v")
+        scale_first(0, 0)
+        scale_first(1, 0)
+        turn_pair(0, 1)
+        quant_x(0, 0, 0, 256)
+        quant_x(0, 1, 0, 256)
         nc.vector.tensor_copy(out=gh[:], in_=gh_bf[:])
-        nc.vector.tensor_scalar(root_i[:], ident[:], ROOT, None, ALU.mult)
+        spread_scale(0)
+        spread_scale(1)
+        spread_k(0)
+        spread_k(1)
+        project(0, 0, 0)
+        project(0, 0, 1)
+        scale_first(0, 1)
+        scale_first(1, 1)
+        quant_x(0, 0, 256, 512)
+        quant_x(0, 1, 256, 512)
         widen(1, 0)
-        quant_x(0, 0)
-        quant_x(0, 1)
-        for j in range(PACK):
-            project(0, 0, j)
 
         open_banks = {}
 
@@ -250,6 +296,7 @@ def tile_extendedinfomaxnaturalgradient_w8_kernel(tc, x_bytes, x_scale, w_words,
                         open_banks[mi, n0] = psum.tile([P, 1, BANK], F32, name="wk")
                     cross_pass(open_banks[mi, n0][:, 0, :], mi, n0, BANK, qq)
 
+        nc.vector.tensor_scalar(root_i[:], ident[:], ROOT, None, ALU.mult)
         late = None
         done = []
         for s, (b, q) in enumerate(steps):
@@ -259,13 +306,22 @@ def tile_extendedinfomaxnaturalgradient_w8_kernel(tc, x_bytes, x_scale, w_words,
             if b == 0:
                 more = q + 1 < NG
                 scalar_e(b, q, 0)
+                if s == 0:
+                    scalar_e(b, q, 1)
+                    project(0, 0, 2)
+                    project(0, 0, 3)
                 if more:
                     widen(q + 1, 1)
                     turn_pair(q + 1, 0)
                 if late:
                     quant("p", *late)
+                if not more:
+                    inter("p", *prev, "v", 0, CUT3)
+                    if CUT3 < 512:
+                        inter("p", *prev, "s", CUT3, 512)
                 vec_a(b, q, 0)
-                scalar_e(b, q, 1)
+                if s:
+                    scalar_e(b, q, 1)
                 if prev:
                     inter("z", *prev, "s", 0, 256)
                 if more:
@@ -291,7 +347,7 @@ def tile_extendedinfomaxnaturalgradient_w8_kernel(tc, x_bytes, x_scale, w_words,
                     project(*follow, 0)
                     project(*follow, 1)
                     project(*follow, 2)
-                if prev:
+                if more and prev:
                     inter("p", *prev, "s", 0, 256)
                     inter("p", *prev, "s", 256, 512)
                 vec_a(b, q, 3)
@@ -314,7 +370,10 @@ def tile_extendedinfomaxnaturalgradient_w8_kernel(tc, x_bytes, x_scale, w_words,
                 scalar_e(b, q, 0)
                 if not follow:
                     inter("p", *prev, "v", 0, w)
-                inter("z", *prev, "v", 0, w)
+                zc = w * ZSHARE // 16 if follow else w
+                inter("z", *prev, "v", 0, zc)
+                if zc < w:
+                    inter("z", *prev, "s", zc, w)
                 if late:
                     quant("p", *late)
                 scalar_e(b, q, 1)

@@ -37,7 +37,6 @@ def tile_extendedinfomaxnaturalgradient_w8_kernel(tc, x_bytes, x_scale, w_words,
         keep = ctx.enter_context(tc.tile_pool(name="keep", bufs=1))
         work = ctx.enter_context(tc.tile_pool(name="work", bufs=2))
         psum = ctx.enter_context(tc.psum_pool(name="psum", bufs=4))
-        ctx.enter_context(tc.manual_schedule())
 
         warm = keep.tile([P, 1], F32, name="warm")
         nc.vector.memset(warm[:], 0.0)

@@ -26,9 +26,7 @@ ALU = mybir.AluOpType
 ACT = mybir.ActivationFunctionType
 
 BLOCKS = [(0, 512), (512, 256), (768, 256)]
-ZSHARE = 16
-CUT3 = 512
-SHARE = 4
+Z0, P0, Z1, P1, Z2, P2 = 0, 0, 12, 0, 16, 4
 
 
 def tile_extendedinfomaxnaturalgradient_w8_kernel(tc, x_bytes, x_scale, w_words, w_scales, k, g, h, out):
@@ -240,19 +238,20 @@ def tile_extendedinfomaxnaturalgradient_w8_kernel(tc, x_bytes, x_scale, w_words,
                 nc.vector.tensor_scalar(o[:], bank[:], -1.0 / ROOT, None, ALU.mult)
             return o, mi, n0, nw
 
-        def store(o, mi, n0, nw):
+        def store(o, mi, n0, nw, eng=nc.gpsimd):
             nm = BANK // nw
             for a in range(nm):
                 d = (mi + a) * P - n0
                 if 0 <= d < nw:
-                    nc.vector.tensor_tensor(o[:, a, d:d + P], o[:, a, d:d + P], root_i[:], ALU.add)
+                    eng.tensor_tensor(o[:, a, d:d + P], o[:, a, d:d + P], root_i[:], ALU.add)
             nc.sync.dma_start(
                 out=out[mi * P:(mi + nm) * P, n0:n0 + nw].rearrange("(a m) n -> m a n", m=P), in_=o[:])
 
-        steps = [(b, q) for b in range(len(BLOCKS)) for q in range(NG)]
+        steps = [(b, q) for q in range(NG) for b in (0, 1)] + [(2, q) for q in range(NG)]
         jobs = {
-            5: [(0, 0, 512, "s")], 6: [(1, 0, 512, "s"), (2, 0, 512, "s")], 7: [(3, 0, 512, "s")],
-            9: [(0, 512, 256, "s"), (2, 512, 256, "s"), (4, 512, 256, "s")], 10: [(4, 0, 512, "s"), (5, 0, 512, "s")],
+            8: [(0, 0, 512, "s"), (1, 0, 512, "s")],
+            9: [(2, 0, 512, "s"), (3, 0, 512, "s"), (0, 512, 256, "s")],
+            10: [(2, 512, 256, "s"), (4, 0, 512, "s"), (5, 0, 512, "s"), (4, 512, 256, "s")],
         }
 
         def turn_pair(q, pair):
@@ -273,7 +272,7 @@ def tile_extendedinfomaxnaturalgradient_w8_kernel(tc, x_bytes, x_scale, w_words,
         turn_pair(0, 1)
         quant_x(0, 0, 0, 256)
         quant_x(0, 1, 0, 256)
-        nc.vector.tensor_copy(out=gh[:], in_=gh_bf[:])
+        nc.gpsimd.tensor_copy(out=gh[:], in_=gh_bf[:])
         spread_scale(0)
         spread_scale(1)
         spread_k(0)
@@ -288,101 +287,94 @@ def tile_extendedinfomaxnaturalgradient_w8_kernel(tc, x_bytes, x_scale, w_words,
 
         open_banks = {}
 
-        def open_all(qq):
-            for mi in (6, 7):
-                for n0 in (0, 512):
-                    if qq == 0:
-                        open_banks[mi, n0] = psum.tile([P, 1, BANK], F32, name="wk")
-                    cross_pass(open_banks[mi, n0][:, 0, :], mi, n0, BANK, qq)
+        def open_pass(mi, n0, qq):
+            if qq == 0:
+                open_banks[mi, n0] = psum.tile([P, 1, BANK], F32, name="wk")
+            cross_pass(open_banks[mi, n0][:, 0, :], mi, n0, BANK, qq)
 
-        nc.vector.tensor_scalar(root_i[:], ident[:], ROOT, None, ALU.mult)
+        nc.gpsimd.tensor_scalar(root_i[:], ident[:], ROOT, 0.0, ALU.mult, ALU.add)
+
+        def inter_both(kind, step, share):
+            w = BLOCKS[step[0]][1]
+            cut = w * share // 16
+            if cut:
+                inter(kind, *step, "v", 0, cut)
+            if cut < w:
+                inter(kind, *step, "s", cut, w)
+
         late = None
         done = []
         for s, (b, q) in enumerate(steps):
             prev = steps[s - 1] if s else None
             follow = steps[s + 1] if s + 1 < len(steps) else None
             start_e(b, q)
+            more = b < 2 and q + 1 < NG
             if b == 0:
-                more = q + 1 < NG
                 scalar_e(b, q, 0)
                 if s == 0:
                     scalar_e(b, q, 1)
                     project(0, 0, 2)
                     project(0, 0, 3)
-                if more:
-                    widen(q + 1, 1)
-                    turn_pair(q + 1, 0)
+                if more and s:
+                    widen(q + 1, 0)
                 if late:
                     quant("p", *late)
-                if not more:
-                    inter("p", *prev, "v", 0, CUT3)
-                    if CUT3 < 512:
-                        inter("p", *prev, "s", CUT3, 512)
                 vec_a(b, q, 0)
                 if s:
                     scalar_e(b, q, 1)
-                if prev:
-                    inter("z", *prev, "s", 0, 256)
+                    inter_both("z", prev, Z0)
                 if more:
-                    untank_pair(q + 1, 0)
-                    widen(q + 1, 2)
+                    widen(q + 1, 1)
+                    turn_pair(q + 1, 0)
                 vec_p(b, q, 0)
                 vec_a(b, q, 1)
                 scalar_e(b, q, 2)
-                if prev:
-                    inter("z", *prev, "s", 256, 512)
                 if more:
-                    widen(q + 1, 3)
-                    turn_pair(q + 1, 1)
-                    untank_pair(q + 1, 1)
+                    widen(q + 1, 2)
                 vec_p(b, q, 1)
                 vec_a(b, q, 2)
-                if more:
-                    quant_x(q + 1, 0)
-                scalar_e(b, q, 3)
-                vec_p(b, q, 2)
-                if more:
-                    quant_x(q + 1, 1)
-                    project(*follow, 0)
-                    project(*follow, 1)
-                    project(*follow, 2)
-                if more and prev:
-                    inter("p", *prev, "s", 0, 256)
-                    inter("p", *prev, "s", 256, 512)
-                vec_a(b, q, 3)
-                if q + 2 < NG:
-                    widen(q + 2, 0)
                 if prev:
                     quant("z", *prev)
-                vec_p(b, q, 3)
+                scalar_e(b, q, 3)
                 if more:
-                    project(*follow, 3)
-                else:
-                    project(*follow, 0)
-                    project(*follow, 1)
+                    widen(q + 1, 3)
+                    untank_pair(q + 1, 0)
+                    turn_pair(q + 1, 1)
+                vec_p(b, q, 2)
+                vec_a(b, q, 3)
+                project(*follow, 0)
+                project(*follow, 1)
+                if prev:
+                    inter_both("p", prev, P0)
+                vec_p(b, q, 3)
             else:
                 for item in done:
                     store(*item)
                 done = []
-                w = BLOCKS[prev[0]][1]
-                cut = w * SHARE // 16 if follow else w
+                zs, ps = (Z1, P1) if b == 1 else (Z2, P2) if follow else (16, 16)
                 scalar_e(b, q, 0)
+                scalar_e(b, q, 1)
+                if more:
+                    untank_pair(q + 1, 1)
                 if not follow:
-                    inter("p", *prev, "v", 0, w)
-                zc = w * ZSHARE // 16 if follow else w
-                inter("z", *prev, "v", 0, zc)
-                if zc < w:
-                    inter("z", *prev, "s", zc, w)
+                    inter_both("p", prev, ps)
+                inter_both("z", prev, zs)
                 if late:
                     quant("p", *late)
-                scalar_e(b, q, 1)
-                if not follow:
-                    open_all(0)
-                    open_all(1)
-                    inter("z", *steps[s], "s", 0, BLOCKS[b][1])
                 vec_a(b, q, 0)
+                if not follow:
+                    open_pass(6, 0, 0)
+                    open_pass(6, 0, 1)
+                    open_pass(6, 512, 0)
+                    open_pass(6, 512, 1)
+                    inter("z", b, q, "s", 0, BLOCKS[b][1])
                 vec_a(b, q, 1)
                 vec_p(b, q, 0)
+                if more:
+                    quant_x(q + 1, 0)
+                    quant_x(q + 1, 1)
+                    project(*follow, 0)
+                    project(*follow, 1)
                 vec_a(b, q, 2)
                 vec_p(b, q, 1)
                 quant("z", *prev)
@@ -391,25 +383,27 @@ def tile_extendedinfomaxnaturalgradient_w8_kernel(tc, x_bytes, x_scale, w_words,
                 vec_a(b, q, 3)
                 vec_p(b, q, 2)
                 if follow:
-                    if cut:
-                        inter("p", *prev, "v", 0, cut)
-                    inter("p", *prev, "s", cut, w)
+                    inter_both("p", prev, ps)
                 else:
-                    quant("z", *steps[s])
+                    quant("z", b, q)
                 vec_p(b, q, 3)
                 if follow:
-                    project(*follow, 0)
-                    project(*follow, 1)
+                    project(*follow, 2 if more else 0)
+                    project(*follow, 3 if more else 1)
                 for mi, n0, nw, eng in jobs.get(s, []):
                     done.append(leave(cross(mi, n0, nw), mi, n0, nw, eng))
             late = prev
         last = steps[-1]
         w = BLOCKS[-1][1]
-        open_all(2)
+        open_pass(6, 0, 2)
+        open_pass(6, 512, 2)
+        for n0 in (0, 512):
+            for qq in range(NG - 1):
+                open_pass(7, n0, qq)
         inter("p", *last, "v", 0, w)
         quant("p", *last)
         for i, mi in enumerate((0, 2, 4)):
             store(*leave(cross(mi, 768, 256, "y"), mi, 768, 256, "sv"[i % 2]))
-        for i, (mi, n0) in enumerate(open_banks):
+        for i, (mi, n0) in enumerate(((6, 512), (7, 512), (6, 0), (7, 0))):
             cross_pass(open_banks[mi, n0][:, 0, :], mi, n0, BANK, NG - 1)
-            store(*leave(open_banks[mi, n0], mi, n0, BANK, "vs"[i % 2]))
+            store(*leave(open_banks[mi, n0], mi, n0, BANK, "vs"[i % 2]), nc.vector)

import math
from contextlib import ExitStack

import concourse.mybir as mybir
from concourse.masks import make_identity

N, D = 2048, 1024
P = 128
PACK = 4
GROUP = P * PACK
NG = N // GROUP
KG = D // GROUP
BANK = 512
ROOT = math.sqrt(N)

FLOPS = 4 * N * D * D

F32 = mybir.dt.float32
BF16 = mybir.dt.bfloat16
U32 = mybir.dt.uint32
I32 = mybir.dt.int32
U8 = mybir.dt.uint8
FP8 = mybir.dt.float8_e4m3fn
X4 = mybir.dt.float8_e4m3fn_x4
ALU = mybir.AluOpType
ACT = mybir.ActivationFunctionType

BLOCKS = [(0, 512), (512, 256), (768, 256)]
Z0, P0, Z1, P1, Z2, P2 = 0, 0, 12, 0, 16, 4


def tile_extendedinfomaxnaturalgradient_w8_kernel(tc, x_bytes, x_scale, w_words, w_scales, k, g, h, out):
    nc = tc.nc
    with ExitStack() as ctx:
        keep = ctx.enter_context(tc.tile_pool(name="keep", bufs=1))
        work = ctx.enter_context(tc.tile_pool(name="work", bufs=2))
        psum = ctx.enter_context(tc.psum_pool(name="psum", bufs=4))

        warm = keep.tile([P, 1], F32, name="warm")
        nc.vector.memset(warm[:], 0.0)
        warm_out = keep.tile([P, 1], F32, name="warm_out")
        nc.scalar.activation(warm_out[:], warm[:], ACT.Tanh)

        w_sc = keep.tile([P, KG, D], U8, name="w_sc", align_bytes=64)
        nc.vector.memset(w_sc[:].rearrange("p g n -> p (g n)").bitcast(I32), 0)

        ident = keep.tile([P, P], F32, name="ident")
        make_identity(nc, ident[:])

        k_row = keep.tile([P, D], BF16, name="k_row")
        nc.vector.memset(k_row[:].bitcast(I32), 0)
        nc.scalar.dma_start(out=k_row[0:1, :], in_=k.rearrange("(o n) -> o n", o=1))
        gh_bf = keep.tile([P, 2, NG, PACK], BF16, name="gh_bf")
        with nc.allow_non_contiguous_dma(reason="gains: four neighbouring samples a piece"):
            nc.scalar.dma_start(out=gh_bf[:, 0], in_=g.rearrange("(q m t) -> m q t", m=P, t=PACK))
            nc.scalar.dma_start(out=gh_bf[:, 1], in_=h.rearrange("(q m t) -> m q t", m=P, t=PACK))
        ones = keep.tile([P, P], BF16, name="ones")
        nc.vector.memset(ones[:], 1.0)
        k_bc = keep.tile([P, D], BF16, name="k_bc")

        x_view = x_bytes.rearrange("(q m t) k -> q m (t k)", m=P, t=PACK)
        xb = [keep.tile([P, PACK * D], U8, name=f"xb{q}") for q in range(NG)]
        half = PACK * D // 2
        xs = keep.tile([P, D], F32, name="xs")
        w_codes = keep.tile([P, KG, D], U32, name="w_codes", align_bytes=64)
        w_view = [w_words[c].rearrange("p n t -> p (n t)").bitcast(I32) for c in range(KG)]
        xs_col = keep.tile([P, KG, PACK], F32, name="xs_col")
        for t in range(PACK // 2):
            nc.sync.dma_start(out=xb[0][:, t * D:(t + 1) * D], in_=x_view[0][:, t * D:(t + 1) * D])
        nc.sync.dma_start(out=xs_col[:], in_=x_scale.rearrange("o (c p t) -> p (o c) t", p=P, t=PACK))
        nc.sync.dma_start(out=xb[0][:, half:], in_=x_view[0][:, half:])
        for j in range(PACK):
            nc.sync.dma_start(
                out=w_sc[j:P:32, :, :].bitcast(I32),
                in_=w_scales[:, j:16:4, :].rearrange("c q n -> q c n").bitcast(I32))
        for c in range(KG):
            nc.sync.dma_start(out=w_codes[:, c, :BANK].bitcast(I32), in_=w_view[c][:, :BANK])
        nc.sync.dma_start(out=xb[1][:], in_=x_view[1])
        for c in range(KG):
            nc.sync.dma_start(out=w_codes[:, c, BANK:].bitcast(I32), in_=w_view[c][:, BANK:])
        for q in range(2, NG):
            nc.sync.dma_start(out=xb[q][:], in_=x_view[q])

        gh = keep.tile([P, 2, NG, PACK], F32, name="gh")
        root_i = keep.tile([P, P], F32, name="root_i")

        x_codes = [keep.tile([P, KG, GROUP], U32, name=f"x_codes{q}", align_bytes=64) for q in range(NG)]
        x_sc = [keep.tile([P, KG, GROUP], U8, name=f"x_sc{q}", align_bytes=64) for q in range(NG)]
        p_codes = keep.tile([P, NG, D], U32, name="p_codes", align_bytes=64)
        p_sc = keep.tile([P, NG, D], U8, name="p_sc", align_bytes=64)
        z_codes = keep.tile([P, NG, D], U32, name="z_codes", align_bytes=64)
        z_sc = keep.tile([P, NG, D], U8, name="z_sc", align_bytes=64)

        xv = {}
        xg = {}

        def widen(q, t):
            xv[q, t] = work.tile([P, D], BF16, name="xv", bufs=6)
            nc.vector.tensor_tensor(xv[q, t][:], xb[q][:, t * D:(t + 1) * D].bitcast(FP8), xs[:], ALU.mult)

        xt = {}

        def turn(q, c, pair):
            b = psum.tile([P, 2, 2 * P], F32, name="wk")
            for a in range(2):
                words = xv[q, 2 * pair + a][:].bitcast(F32)
                for u in range(2):
                    nc.tensor.transpose(b[:, u, a * P:(a + 1) * P], words[:, 256 * c + u:256 * (c + 1):2], ident[:])
            xt[q, c, pair] = b

        def grouped(q, c, pair):
            if pair == 0:
                xg[q, c] = work.tile([P, GROUP * PACK], BF16, name=f"xg{c}", align_bytes=64)
            return xg[q, c][:, pair * 1024:(pair + 1) * 1024]

        def untank(q, c, pair):
            dst = grouped(q, c, pair).bitcast(F32)
            nc.scalar.copy(dst.rearrange("p (r u) -> p r u", u=2), xt[q, c, pair][:].rearrange("p u r -> p r u"))

        def widen_first(t, eng):
            xv[0, t] = work.tile([P, D], BF16, name="xv", bufs=6)
            byte = xb[0][:, t * D:(t + 1) * D].bitcast(FP8)
            if eng == "s":
                nc.scalar.copy(xv[0, t][:], byte)
            else:
                nc.vector.tensor_copy(out=xv[0, t][:], in_=byte)

        def scale_first(c, pair):
            nc.vector.tensor_tensor(
                grouped(0, c, pair).rearrange("p (r u e) -> p r u e", u=2, e=2),
                xt[0, c, pair][:].bitcast(BF16).rearrange("p u (r e) -> p r u e", e=2),
                xs_col[:, c, :].rearrange("p (o u e) -> p o u e", o=1, u=2).broadcast_to([P, 2 * P, 2, 2]),
                ALU.mult)

        def spread_scale(c):
            bank = psum.tile([P, PACK, P], F32, name="y")
            for t in range(PACK):
                nc.tensor.matmul(bank[:, t, :], lhsT=xs_col[:, c, t:t + 1].to_broadcast([P, P]), rhs=ident[:], start=True, stop=True)
            nc.scalar.copy(
                xs[:, c * GROUP:(c + 1) * GROUP].rearrange("p (n t) -> p n t", t=PACK), bank[:].rearrange("p t n -> p n t"))

        def spread_k(c):
            bank = psum.tile([P, BANK], F32, name="y")
            nc.tensor.matmul(bank[:], lhsT=ones[:], rhs=k_row[:, c * BANK:(c + 1) * BANK], start=True, stop=True)
            nc.scalar.copy(k_bc[:, c * BANK:(c + 1) * BANK], bank[:])

        def quant_x(q, c, lo=0, hi=GROUP):
            nc.vector.quantize_mx(
                out=x_codes[q][:, c, lo:hi].bitcast(X4), scales=x_sc[q][:, c, lo:hi], in_=xg[q, c][:, lo * PACK:hi * PACK])

        y = {}
        th = {}
        aa = {}
        pp = {}
        zp = {}
        pi = {}
        zi = {}

        def project(b, q, j):
            c0, cw = BLOCKS[b]
            nt = BANK // cw
            bank = psum.tile([P, nt, cw], F32, name="y", bufs=4)
            for a in range(nt):
                t = j * nt + a
                for c in range(KG):
                    nc.tensor.matmul_mx(
                        out=bank[:, a, :],
                        lhsT=x_codes[q][:, c, t * P:(t + 1) * P].bitcast(X4),
                        lhsT_scale=x_sc[q][:, c, t * P:(t + 1) * P],
                        rhs=w_codes[:, c, c0:c0 + cw].bitcast(X4),
                        rhs_scale=w_sc[:, c, c0:c0 + cw],
                        start=(c == 0), stop=(c == KG - 1))
                y[b, q, t] = bank[:, a, :]
            y[b, q, "bank", j] = bank

        def start_e(b, q):
            cw = BLOCKS[b][1]
            pp[b, q] = work.tile([P, PACK, cw], BF16, name="pp", bufs=3, align_bytes=64)
            zp[b, q] = work.tile([P, PACK, cw], BF16, name="zp", bufs=3, align_bytes=64)

        def scalar_e(b, q, j):
            cw = BLOCKS[b][1]
            nt = BANK // cw
            tt = work.tile([P, nt, cw], F32, name="th", bufs=4)
            nc.scalar.activation(tt[:], y[b, q, "bank", j][:], ACT.Tanh)
            for a in range(nt):
                t = j * nt + a
                th[b, q, t] = tt[:, a, :]
                nc.scalar.activation(zp[b, q][:, t, :], y[b, q, t], ACT.Copy, scale=gh[:, 1, q, t:t + 1])

        def vec_a(b, q, t):
            c0, cw = BLOCKS[b][0], BLOCKS[b][1]
            a = work.tile([P, cw], F32, name="aa", bufs=4)
            nc.vector.scalar_tensor_tensor(a[:], th[b, q, t], gh[:, 0, q, t:t + 1], k_bc[:, c0:c0 + cw], ALU.mult, ALU.mult)
            aa[b, q, t] = a

        def vec_p(b, q, t):
            nc.vector.scalar_tensor_tensor(pp[b, q][:, t, :], y[b, q, t], gh[:, 0, q, t:t + 1], aa[b, q, t][:], ALU.mult, ALU.add)

        def inter(kind, b, q, eng, lo, hi):
            src = (zp if kind == "z" else pp)[b, q]
            dst = zi if kind == "z" else pi
            if (b, q) not in dst:
                dst[b, q] = work.tile([P, BLOCKS[b][1] * PACK], BF16, name=kind + "i", bufs=3, align_bytes=64)
            o = dst[b, q][:, lo * PACK:hi * PACK].rearrange("p (c i t) -> p c t i", i=4, t=PACK)
            s = src[:, :, lo:hi].rearrange("p t (c i) -> p c t i", i=4)
            if eng == "s":
                nc.scalar.copy(o, s)
            else:
                nc.vector.tensor_copy(out=o, in_=s)

        def quant(kind, b, q):
            c0, cw = BLOCKS[b][0], BLOCKS[b][1]
            codes, sc, src = (z_codes, z_sc, zi) if kind == "z" else (p_codes, p_sc, pi)
            nc.vector.quantize_mx(out=codes[:, q, c0:c0 + cw].bitcast(X4), scales=sc[:, q, c0:c0 + cw], in_=src[b, q][:])

        def cross_pass(dst, mi, n0, nw, q):
            nc.tensor.matmul_mx(
                out=dst,
                lhsT=p_codes[:, q, mi * P:(mi + 1) * P].bitcast(X4), lhsT_scale=p_sc[:, q, mi * P:(mi + 1) * P],
                rhs=z_codes[:, q, n0:n0 + nw].bitcast(X4), rhs_scale=z_sc[:, q, n0:n0 + nw],
                start=(q == 0), stop=(q == NG - 1))

        def cross(mi, n0, nw, tag="wk"):
            nm = BANK // nw
            bank = psum.tile([P, nm, nw], F32, name=tag)
            for a in range(nm):
                for q in range(NG):
                    cross_pass(bank[:, a, :], mi + a, n0, nw, q)
            return bank

        def leave(bank, mi, n0, nw, eng):
            nm = BANK // nw
            o = work.tile([P, nm, nw], F32, name="o", bufs=8)
            if eng == "s":
                nc.scalar.activation(o[:], bank[:], ACT.Copy, scale=-1.0 / ROOT)
            else:
                nc.vector.tensor_scalar(o[:], bank[:], -1.0 / ROOT, None, ALU.mult)
            return o, mi, n0, nw

        def store(o, mi, n0, nw, eng=nc.gpsimd):
            nm = BANK // nw
            for a in range(nm):
                d = (mi + a) * P - n0
                if 0 <= d < nw:
                    eng.tensor_tensor(o[:, a, d:d + P], o[:, a, d:d + P], root_i[:], ALU.add)
            nc.sync.dma_start(
                out=out[mi * P:(mi + nm) * P, n0:n0 + nw].rearrange("(a m) n -> m a n", m=P), in_=o[:])

        steps = [(b, q) for q in range(NG) for b in (0, 1)] + [(2, q) for q in range(NG)]
        jobs = {
            8: [(0, 0, 512, "s"), (1, 0, 512, "s")],
            9: [(2, 0, 512, "s"), (3, 0, 512, "s"), (0, 512, 256, "s")],
            10: [(2, 512, 256, "s"), (4, 0, 512, "s"), (5, 0, 512, "s"), (4, 512, 256, "s")],
        }

        def turn_pair(q, pair):
            for c in range(KG):
                turn(q, c, pair)

        def untank_pair(q, pair):
            for c in range(KG):
                untank(q, c, pair)

        widen_first(0, "s")
        widen_first(1, "v")
        turn_pair(0, 0)
        widen_first(2, "s")
        widen_first(3, "v")
        scale_first(0, 0)
        scale_first(1, 0)
        turn_pair(0, 1)
        quant_x(0, 0, 0, 256)
        quant_x(0, 1, 0, 256)
        nc.gpsimd.tensor_copy(out=gh[:], in_=gh_bf[:])
        spread_scale(0)
        spread_scale(1)
        spread_k(0)
        spread_k(1)
        project(0, 0, 0)
        project(0, 0, 1)
        scale_first(0, 1)
        scale_first(1, 1)
        quant_x(0, 0, 256, 512)
        quant_x(0, 1, 256, 512)
        widen(1, 0)

        open_banks = {}

        def open_pass(mi, n0, qq):
            if qq == 0:
                open_banks[mi, n0] = psum.tile([P, 1, BANK], F32, name="wk")
            cross_pass(open_banks[mi, n0][:, 0, :], mi, n0, BANK, qq)

        nc.gpsimd.tensor_scalar(root_i[:], ident[:], ROOT, 0.0, ALU.mult, ALU.add)

        def inter_both(kind, step, share):
            w = BLOCKS[step[0]][1]
            cut = w * share // 16
            if cut:
                inter(kind, *step, "v", 0, cut)
            if cut < w:
                inter(kind, *step, "s", cut, w)

        late = None
        done = []
        for s, (b, q) in enumerate(steps):
            prev = steps[s - 1] if s else None
            follow = steps[s + 1] if s + 1 < len(steps) else None
            start_e(b, q)
            more = b < 2 and q + 1 < NG
            if b == 0:
                scalar_e(b, q, 0)
                if s == 0:
                    scalar_e(b, q, 1)
                    project(0, 0, 2)
                    project(0, 0, 3)
                if more and s:
                    widen(q + 1, 0)
                if late:
                    quant("p", *late)
                vec_a(b, q, 0)
                if s:
                    scalar_e(b, q, 1)
                    inter_both("z", prev, Z0)
                if more:
                    widen(q + 1, 1)
                    turn_pair(q + 1, 0)
                vec_p(b, q, 0)
                vec_a(b, q, 1)
                scalar_e(b, q, 2)
                if more:
                    widen(q + 1, 2)
                vec_p(b, q, 1)
                vec_a(b, q, 2)
                if prev:
                    quant("z", *prev)
                scalar_e(b, q, 3)
                if more:
                    widen(q + 1, 3)
                    untank_pair(q + 1, 0)
                    turn_pair(q + 1, 1)
                vec_p(b, q, 2)
                vec_a(b, q, 3)
                project(*follow, 0)
                project(*follow, 1)
                if prev:
                    inter_both("p", prev, P0)
                vec_p(b, q, 3)
            else:
                for item in done:
                    store(*item)
                done = []
                zs, ps = (Z1, P1) if b == 1 else (Z2, P2) if follow else (16, 16)
                scalar_e(b, q, 0)
                scalar_e(b, q, 1)
                if more:
                    untank_pair(q + 1, 1)
                if not follow:
                    inter_both("p", prev, ps)
                inter_both("z", prev, zs)
                if late:
                    quant("p", *late)
                vec_a(b, q, 0)
                if not follow:
                    open_pass(6, 0, 0)
                    open_pass(6, 0, 1)
                    open_pass(6, 512, 0)
                    open_pass(6, 512, 1)
                    inter("z", b, q, "s", 0, BLOCKS[b][1])
                vec_a(b, q, 1)
                vec_p(b, q, 0)
                if more:
                    quant_x(q + 1, 0)
                    quant_x(q + 1, 1)
                    project(*follow, 0)
                    project(*follow, 1)
                vec_a(b, q, 2)
                vec_p(b, q, 1)
                quant("z", *prev)
                if not follow:
                    quant("p", *prev)
                vec_a(b, q, 3)
                vec_p(b, q, 2)
                if follow:
                    inter_both("p", prev, ps)
                else:
                    quant("z", b, q)
                vec_p(b, q, 3)
                if follow:
                    project(*follow, 2 if more else 0)
                    project(*follow, 3 if more else 1)
                for mi, n0, nw, eng in jobs.get(s, []):
                    done.append(leave(cross(mi, n0, nw), mi, n0, nw, eng))
            late = prev
        last = steps[-1]
        w = BLOCKS[-1][1]
        open_pass(6, 0, 2)
        open_pass(6, 512, 2)
        for n0 in (0, 512):
            for qq in range(NG - 1):
                open_pass(7, n0, qq)
        inter("p", *last, "v", 0, w)
        quant("p", *last)
        for i, mi in enumerate((0, 2, 4)):
            store(*leave(cross(mi, 768, 256, "y"), mi, 768, 256, "sv"[i % 2]))
        for i, (mi, n0) in enumerate(((6, 512), (7, 512), (6, 0), (7, 0))):
            cross_pass(open_banks[mi, n0][:, 0, :], mi, n0, BANK, NG - 1)
            store(*leave(open_banks[mi, n0], mi, n0, BANK, "vs"[i % 2]), nc.vector)
